import numpy as np
import ml_dtypes


def mxq(x, axis, fmt="e4m3"):
    dtype, down = {"e4m3": (ml_dtypes.float8_e4m3fn, 7), "e5m2": (ml_dtypes.float8_e5m2, 14)}[fmt]
    v = np.moveaxis(np.asarray(x, np.float32).astype(ml_dtypes.bfloat16).astype(np.float64), axis, -1)
    blocks = v.reshape(v.shape[:-1] + (-1, 32))
    amax = np.abs(blocks).max(-1, keepdims=True)
    byte = np.maximum(np.where(amax > 0, np.frexp(amax)[1] - 1 + 127, 0) - down, 1)
    scale = np.exp2(byte - 127.0)
    codes = (blocks / scale).astype(np.float32).astype(dtype).astype(np.float64)
    return np.moveaxis((codes * scale).reshape(v.shape), -1, axis)


WIDE = False


def mx_kscale(k):
    if not WIDE:
        return np.ones(k)
    levels = np.array([10, -10, 5, -5, 0])
    if k % 512:
        return np.exp2(np.random.permutation(np.resize(levels, k // 32))).repeat(32)
    a = np.empty((k // 512, 16))
    for p in range(k // 512):
        a[p, :8] = np.random.permutation(np.resize(levels, 8))
        for g in range(8):
            far = levels[np.abs(levels - a[p, g]) >= 10]
            a[p, g + 8] = far[np.random.randint(len(far))]
    return np.exp2(a.ravel()).repeat(32)


BF16 = ml_dtypes.bfloat16


def bf(x):
    return np.asarray(x, np.float32).astype(BF16)


def f64(x):
    return np.asarray(x).astype(np.float64)


E2M1 = np.array([0.0, 0.5, 1.0, 1.5, 2.0, 3.0, 4.0, 6.0, -0.0, -0.5, -1.0, -1.5, -2.0, -3.0, -4.0, -6.0])


def pack_weight(w, fmt):
    k, n = w.shape
    w = f64(bf(w)).reshape(k // 32, 32, n)
    amax = np.abs(w).max(1)
    if fmt == "e4m3":
        byte = np.frexp(amax)[1] - 1 + 127 - 7
    else:
        mant, ex = np.frexp(amax / 6.0)
        byte = np.where(mant > 0.5, ex, ex - 1) + 127
    byte = np.clip(np.where(amax > 0, byte, 1), 1, 254)
    scaled = (w * np.exp2(127.0 - byte)[:, None, :]).reshape(k, n).astype(np.float32)
    by_word = np.ascontiguousarray(scaled.reshape(k // 512, 128, 4, n).transpose(0, 1, 3, 2))
    if fmt == "e4m3":
        words = by_word.astype(ml_dtypes.float8_e4m3fn).view(np.uint8)
    else:
        c = by_word.astype(ml_dtypes.float4_e2m1fn).view(np.uint8) & 0xF
        words = c[..., 0::2] | (c[..., 1::2] << 4)
    return np.ascontiguousarray(words), np.ascontiguousarray(byte.astype(np.uint8).reshape(k // 512, 16, n))


def unpack_weight(words, scales, fmt):
    g, p, n, _ = words.shape
    if fmt == "e4m3":
        vals = np.ascontiguousarray(words).view(ml_dtypes.float8_e4m3fn).astype(np.float64)
    else:
        nib = np.empty((g, p, n, 4), np.uint8)
        nib[..., 0::2] = words & 0xF
        nib[..., 1::2] = words >> 4
        vals = E2M1[nib]
    vals = vals * np.repeat(np.exp2(scales.astype(np.float64) - 127.0), 8, axis=1)[..., None]
    return vals.transpose(0, 1, 3, 2).reshape(g * 512, n)
def pack4(w):
    words, scales = pack_weight(w, "e2m1")
    return words.reshape(words.shape[0], 128, -1), scales


def unpack4(words, scales):
    return unpack_weight(words.reshape(words.shape[0], 128, -1, 2), scales, "e2m1")


E4M3FN = np.array([(-1.0 if i & 128 else 1.0) * ((1.0 + (i & 7) / 8.0) * 2.0 ** (((i >> 3) & 15) - 7) if i & 120 else (i & 7) * 2.0 ** -9) for i in range(256)])


def e4m3fn_bytes(y):
    return np.clip(np.asarray(y, np.float64), -448.0, 448.0).astype(np.float32).astype(ml_dtypes.float8_e4m3fn).view(np.uint8)


def e4m3fn_values(b):
    return E4M3FN[b]


F, J, D, A, H, T = 1024, 1024, 1024, 512, 4, 512


def scale_heads(q, head_w):
    n_feat, n_cols = q.shape
    n_heads = head_w.shape[0]
    per_head = q.reshape(n_feat, n_heads, n_cols // n_heads)
    return (per_head * head_w[None, :, None]).reshape(n_feat, n_cols)


def draw0():
    s, u = mx_kscale(D), mx_kscale(D)
    t = mx_kscale(A)
    r = mx_kscale(T)
    dq = bf(np.random.standard_normal((F, D)) * s)
    dk = bf(np.random.standard_normal((J, D)) * u)
    wq_words, wq_scales = pack4(np.random.standard_normal((D, A)) / np.sqrt(D) / s[:, None] * t)
    wk_words, wk_scales = pack4(np.random.standard_normal((D, A)) / np.sqrt(D) / u[:, None] / t)
    return {
        "dq": dq,
        "dk": dk,
        "wq_words": wq_words,
        "wq_scales": wq_scales,
        "wk_words": wk_words,
        "wk_scales": wk_scales,
        "head_w": bf(1.0 + 0.25 * np.random.standard_normal(H)),
        "aq": bf(np.random.standard_normal((T, F)) * T**0.25 * r[:, None]),
        "ak": bf(np.random.standard_normal((T, J)) * T**0.25 / r[:, None]),
        "g": bf(np.random.standard_normal(T)),
    }


def core(dq, dk, wq_words, wq_scales, wk_words, wk_scales, head_w, aq, ak, g):
    n_pairs = aq.shape[0]
    head_dim = wq_scales.shape[2] // head_w.shape[0]

    q = mxq(f64(dq), 1, "e4m3") @ unpack4(wq_words, wq_scales)
    k = mxq(f64(dk), 1, "e4m3") @ unpack4(wk_words, wk_scales)

    qw = scale_heads(q, f64(head_w))

    m = (mxq(qw, 1, "e4m3") @ mxq(k.T, 0, "e4m3")) / np.sqrt(head_dim)

    c = (mxq(f64(aq).T, 1, "e4m3") @ mxq(f64(g)[:, None] * f64(ak), 0, "e4m3")) / n_pairs

    return m * c


def setup_inputs():
    drawn = draw0()
    full = np.asarray(drawn['dq']).astype(np.float64)
    scale = (np.abs(full).reshape(8, 128, 8, 128).max(axis=(1, 3)) / 448.0).astype(np.float32)
    given = {}
    for key, value in drawn.items():
        if key == 'dq':
            given['dq_bytes'] = e4m3fn_bytes(full / np.repeat(np.repeat(scale.astype(np.float64), 128, axis=0), 128, axis=1))
            given['dq_scale'] = scale
        else:
            given[key] = value
    return given


def reference(dq_bytes, dq_scale, dk, wq_words, wq_scales, wk_words, wk_scales, head_w, aq, ak, g):
    return core(e4m3fn_values(dq_bytes) * np.repeat(np.repeat(dq_scale.astype(np.float64), 128, axis=0), 128, axis=1), dk, wq_words, wq_scales, wk_words, wk_scales, head_w, aq, ak, g)

@@ -1,0 +1,295 @@
+import math
+from contextlib import ExitStack
+
+import concourse.mybir as mybir
+from concourse.masks import make_identity
+
+F, J, D, A, H, T = 1024, 1024, 1024, 512, 4, 512
+FLOPS = 2 * (2 * 1024 * D * A + F * J * A + F * J * T)
+
+F32 = mybir.dt.float32
+BF16 = mybir.dt.bfloat16
+I32 = mybir.dt.int32
+U32 = mybir.dt.uint32
+U8 = mybir.dt.uint8
+FP8 = mybir.dt.float8_e4m3fn
+FP8X4 = mybir.dt.float8_e4m3fn_x4
+FP4X4 = mybir.dt.float4_e2m1fn_x4
+MULT = mybir.AluOpType.mult
+COPY = mybir.ActivationFunctionType.Copy
+P = 128
+
+
+def tile_featurepairqkscoreattribution_d2p_kernel(
+    tc, dq_bytes, dq_scale, dk, wq_words, wq_scales, wk_words, wk_scales, head_w, aq, ak, g, out
+):
+    nc = tc.nc
+    with ExitStack() as ctx:
+        keep = ctx.enter_context(tc.tile_pool(name="keep", bufs=1))
+        work = ctx.enter_context(tc.tile_pool(name="work", bufs=4))
+        psum = ctx.enter_context(tc.psum_pool(name="psum", bufs=8))
+        ctx.enter_context(tc.manual_schedule())
+
+        ident = keep.tile([P, P], F32, name="ident")
+        sc_raw = {}
+        sc = {}
+        wd_raw = {}
+        wd = {}
+        for n in ("k", "q"):
+            sc_raw[n] = keep.tile([P, 256], I32, name="sc_raw_" + n, align_bytes=64)
+            sc[n] = keep.tile([P, 256], I32, name="sc_" + n, align_bytes=64)
+            wd_raw[n] = keep.tile([P, 512], I32, name="wd_raw_" + n, align_bytes=64)
+            wd[n] = keep.tile([P, 512], I32, name="wd_" + n, align_bytes=64)
+        dqs = keep.tile([P, 64], F32, name="dqs")
+        hw4 = keep.tile([P, 4], BF16, name="hw4")
+        hcol = keep.tile([P, 1], F32, name="hcol")
+        gt = keep.tile([P, 4], BF16, name="gt")
+        dk_sb = [keep.tile([P, 2, D], BF16, name="dk_sb%d" % s) for s in range(4)]
+        dq_sb = [keep.tile([P, 2, D], U8, name="dq_sb%d" % s) for s in range(4)]
+        aq_sb = [keep.tile([P, 4, 512], BF16, name="aq_sb%d" % s) for s in range(2)]
+        ak_sb = [keep.tile([P, 4, 512], BF16, name="ak_sb%d" % s) for s in range(2)]
+        c2 = {}
+        s2 = {}
+        for n in ("k", "q", "aq", "ak"):
+            c2[n] = keep.tile([P, 1024], U32, name="c2_" + n, align_bytes=64)
+            s2[n] = keep.tile([P, 1024], U8, name="s2_" + n, align_bytes=64)
+
+        nc.vector.memset(sc_raw["k"][:], 0)
+        nc.vector.memset(sc_raw["q"][:], 0)
+
+        def load_pair(dst, src, s):
+            nc.sync.dma_start(out=dst[s][:], in_=src[256 * s : 256 * s + 256, :].rearrange("(a p) k -> p a k", p=P))
+
+        def load_half(dst, src, h):
+            nc.sync.dma_start(
+                out=dst[h][:], in_=src[:, 512 * h : 512 * h + 512].rearrange("(p t) w -> p t w", t=4)
+            )
+
+        def load_words(n, src):
+            nc.sync.dma_start(
+                out=wd_raw[n][:].rearrange("p (g n) -> p g n", g=2), in_=src.bitcast(I32).rearrange("g p n -> p g n")
+            )
+
+        def load_scales(eng, n, src):
+            v = src.bitcast(I32)
+            for q in range(4):
+                eng.dma_start(
+                    out=sc_raw[n][32 * q : 32 * q + 4, :].rearrange("q (g n) -> q g n", g=2),
+                    in_=v[:, 4 * q : 4 * q + 4, :].rearrange("g q n -> q g n"),
+                )
+
+        load_pair(dk_sb, dk, 0)
+        load_scales(nc.scalar, "k", wk_scales)
+        load_words("k", wk_words)
+        load_pair(dk_sb, dk, 1)
+        load_half(aq_sb, aq, 0)
+        load_pair(dk_sb, dk, 2)
+        load_half(aq_sb, aq, 1)
+        load_pair(dk_sb, dk, 3)
+        load_pair(dq_sb, dq_bytes, 0)
+        load_words("q", wq_words)
+        load_half(ak_sb, ak, 0)
+        load_pair(dq_sb, dq_bytes, 1)
+        load_half(ak_sb, ak, 1)
+        load_pair(dq_sb, dq_bytes, 2)
+        load_pair(dq_sb, dq_bytes, 3)
+
+        make_identity(nc, ident[:])
+        load_scales(nc.gpsimd, "q", wq_scales)
+        nc.gpsimd.dma_start(out=dqs[:], in_=dq_scale.rearrange("i j -> (i j)").partition_broadcast(P))
+        nc.gpsimd.dma_start(out=gt[:], in_=g.rearrange("(p t) -> p t", t=4))
+        nc.gpsimd.dma_start(out=hw4[:], in_=head_w.partition_broadcast(P))
+        for h in range(H):
+            nc.gpsimd.tensor_copy(out=hcol[32 * h : 32 * h + 32, 0:1], in_=hw4[32 * h : 32 * h + 32, h : h + 1])
+
+        def permute(n):
+            nc.vector.tensor_copy(
+                out=wd[n][:].rearrange("p (t b w) -> p t b w", t=4, w=4),
+                in_=wd_raw[n][:].rearrange("p (b t w) -> p t b w", t=4, w=4),
+            )
+            nc.vector.tensor_copy(
+                out=sc[n][:].rearrange("p (t b w) -> p t b w", t=4, w=2),
+                in_=sc_raw[n][:].rearrange("p (b t w) -> p t b w", t=4, w=2),
+            )
+
+        wide = {}
+        banks = {}
+        kt = {}
+        c1 = {}
+        g2 = {}
+
+        def widen(i):
+            wide[i] = work.tile([P, D], BF16, name="wide", bufs=4)
+            for j in range(8):
+                nc.vector.tensor_scalar(
+                    out=wide[i][:, P * j : P * j + P],
+                    in0=dq_sb[i // 2][:, i % 2, P * j : P * j + P].bitcast(FP8),
+                    scalar1=dqs[:, 8 * i + j : 8 * i + j + 1],
+                    scalar2=None,
+                    op0=MULT,
+                )
+
+        def transposes(n, i):
+            src = dk_sb[i // 2][:, i % 2, :] if n == "k" else wide[i][:]
+            words = src.bitcast(F32)
+            bank = psum.tile([P, 512], F32, name="bank")
+            for gg in range(2):
+                for u in range(2):
+                    c = P * (2 * gg + u)
+                    nc.tensor.transpose(bank[:, c : c + P], words[:, 256 * gg + u : 256 * gg + 256 : 2], ident[:])
+            banks[n, i] = bank
+
+        def evac(n, i):
+            kt[n, i] = work.tile([P, 1024], BF16, name="kt", bufs=4, align_bytes=64)
+            nc.scalar.copy(
+                out=kt[n, i][:].bitcast(F32).rearrange("p (g f u) -> p g f u", g=2, u=2),
+                in_=banks[n, i][:].rearrange("p (g u f) -> p g f u", g=2, u=2),
+            )
+
+        def quant1(n, i):
+            cc = work.tile([P, 256], U32, name="c1", bufs=6, align_bytes=64)
+            ss = work.tile([P, 256], U8, name="s1", bufs=6, align_bytes=64)
+            nc.vector.quantize_mx(out=cc[:].bitcast(FP8X4), scales=ss[:], in_=kt[n, i][:])
+            c1[n, i] = (cc, ss)
+
+        def project(n, i):
+            cc, ss = c1[n, i]
+            bank = psum.tile([P, 512], F32, name="bank")
+            for t in range(4):
+                for gg in range(2):
+                    nc.tensor.matmul_mx(
+                        out=bank[:, P * t : P * t + P],
+                        lhsT=wd[n][:, 128 * t + 64 * gg : 128 * t + 64 * gg + 64].bitcast(FP4X4),
+                        lhsT_scale=sc[n][:, 64 * t + 32 * gg : 64 * t + 32 * gg + 32].bitcast(U8),
+                        rhs=cc[:, P * gg : P * gg + P].bitcast(FP8X4),
+                        rhs_scale=ss[:, P * gg : P * gg + P],
+                        start=(gg == 0),
+                        stop=(gg == 1),
+                    )
+            banks[n, i] = bank
+
+        def empty(n, i):
+            if i % 2 == 0:
+                g2[n, i // 2] = work.tile([P, 2, 512], BF16, name="g2", bufs=3, align_bytes=64)
+            dst = g2[n, i // 2][:, i % 2, :].rearrange("p (f t) -> p f t", t=4)
+            src = banks[n, i][:].rearrange("p (t f) -> p f t", t=4)
+            if n == "k":
+                nc.scalar.copy(out=dst, in_=src)
+            else:
+                nc.scalar.activation(out=dst, in_=src, func=COPY, scale=hcol[:, 0:1])
+
+        def quant2(n, s):
+            nc.vector.quantize_mx(
+                out=c2[n][:, 256 * s : 256 * s + 256].bitcast(FP8X4),
+                scales=s2[n][:, 256 * s : 256 * s + 256],
+                in_=g2[n, s][:].rearrange("p a c -> p (a c)"),
+            )
+
+        il = {}
+
+        def inter(n, h, part, src):
+            if part == 0:
+                il[n, h] = work.tile([P, 2048], BF16, name="il", bufs=2, align_bytes=64)
+            nc.vector.tensor_copy(
+                out=il[n, h][:, 1024 * part : 1024 * part + 1024].rearrange("p (w t) -> p w t", t=4),
+                in_=src[:, :, 256 * part : 256 * part + 256].rearrange("p t w -> p w t"),
+            )
+
+        def quant_a(n, h):
+            nc.vector.quantize_mx(
+                out=c2[n][:, 512 * h : 512 * h + 512].bitcast(FP8X4),
+                scales=s2[n][:, 512 * h : 512 * h + 512],
+                in_=il[n, h][:],
+            )
+
+        gk = {}
+
+        def gmul(h):
+            gk[h] = work.tile([P, 4, 512], BF16, name="gk", bufs=2)
+            for t in range(4):
+                nc.vector.tensor_scalar(
+                    out=gk[h][:, t, :], in0=ak_sb[h][:, t, :], scalar1=gt[:, t : t + 1], scalar2=None, op0=MULT
+                )
+
+        fills = []
+        for h in range(2):
+            fills.append(lambda h=h: inter("aq", h, 0, aq_sb[h]))
+            fills.append(lambda h=h: inter("aq", h, 1, aq_sb[h]))
+            fills.append(lambda h=h: quant_a("aq", h))
+        for h in range(2):
+            fills.append(lambda h=h: gmul(h))
+            fills.append(lambda h=h: inter("ak", h, 0, gk[h]))
+            fills.append(lambda h=h: inter("ak", h, 1, gk[h]))
+            fills.append(lambda h=h: quant_a("ak", h))
+
+        def fill(n):
+            for x in range(min(n, len(fills))):
+                fills[0]()
+                fills.remove(fills[0])
+
+        const = 1.0 / (T * math.sqrt(A // H))
+        otile = {}
+
+        def final_mm(i, j):
+            res = []
+            for x, y in (("aq", "ak"), ("q", "k")):
+                bank = psum.tile([P, 512], F32, name="bank")
+                nc.tensor.matmul_mx(
+                    out=bank[:],
+                    lhsT=c2[x][:, P * i : P * i + P].bitcast(FP8X4),
+                    lhsT_scale=s2[x][:, P * i : P * i + P],
+                    rhs=c2[y][:, 512 * j : 512 * j + 512].bitcast(FP8X4),
+                    rhs_scale=s2[y][:, 512 * j : 512 * j + 512],
+                    start=True,
+                    stop=True,
+                )
+                res.append(bank)
+            banks["f", i, j] = res
+
+        def final_ew(i, j):
+            cb, mb = banks["f", i, j]
+            cs = work.tile([P, 512], F32, name="cs", bufs=4)
+            nc.scalar.activation(out=cs[:], in_=cb[:], func=COPY, scale=const)
+            if j == 0:
+                otile[i] = work.tile([P, 1024], F32, name="ot", bufs=4)
+            nc.vector.tensor_tensor(out=otile[i][:, 512 * j : 512 * j + 512], in0=mb[:], in1=cs[:], op=MULT)
+            if i == 7:
+                nc.sync.dma_start(
+                    out=out[P * i : P * i + P, 512 * j : 512 * j + 512], in_=otile[i][:, 512 * j : 512 * j + 512]
+                )
+            elif j == 1:
+                nc.sync.dma_start(out=out[P * i : P * i + P, :], in_=otile[i][:])
+
+        def name_tile(s, a):
+            return ("k" if s < 4 else "q", 2 * (s % 4) + a)
+
+        nfill = {0: 0, 1: 3, 2: 3, 3: 3, 4: 3, 5: 2}
+        for s in range(10):
+            if s < 8:
+                for a in range(2):
+                    transposes(*name_tile(s, a))
+                for a in range(2):
+                    evac(*name_tile(s, a))
+            if s == 0:
+                permute("k")
+            if s == 3:
+                permute("q")
+            if 3 <= s < 7:
+                for a in range(2):
+                    widen(2 * (s - 3) + a)
+            fill(nfill.get(s, 0))
+            if s < 8:
+                for a in range(2):
+                    quant1(*name_tile(s, a))
+            if 1 <= s <= 8:
+                for a in range(2):
+                    project(*name_tile(s - 1, a))
+                for a in range(2):
+                    empty(*name_tile(s - 1, a))
+                quant2("k" if s - 1 < 4 else "q", (s - 1) % 4)
+            if s >= 6:
+                for a in range(2):
+                    i = 2 * (s - 6) + a
+                    for j in range(2):
+                        final_mm(i, j)
+                        final_ew(i, j)

@@ -44,7 +44,8 @@ def tile_featurepairqkscoreattribution_d2p_kernel(
         hw4 = keep.tile([P, 4], BF16, name="hw4")
         hcol = keep.tile([P, 1], F32, name="hcol")
         gt = keep.tile([P, 4], BF16, name="gt")
-        dk_sb = [keep.tile([P, 2, D], BF16, name="dk_sb%d" % s) for s in range(4)]
+        diag = keep.tile([P, 4, P], BF16, name="diag")
+        dk_sb = [keep.tile([P, D], BF16, name="dk_sb%d" % i) for i in range(8)]
         dq_sb = [keep.tile([P, 2, D], U8, name="dq_sb%d" % s) for s in range(4)]
         aq_sb = [keep.tile([P, 4, 512], BF16, name="aq_sb%d" % s) for s in range(2)]
         ak_sb = [keep.tile([P, 4, 512], BF16, name="ak_sb%d" % s) for s in range(2)]
@@ -56,6 +57,9 @@ def tile_featurepairqkscoreattribution_d2p_kernel(
 
         nc.vector.memset(sc_raw["k"][:], 0)
         nc.vector.memset(sc_raw["q"][:], 0)
+
+        def load_one(i):
+            nc.sync.dma_start(out=dk_sb[i][:], in_=dk[P * i : P * i + P, :])
 
         def load_pair(dst, src, s):
             nc.sync.dma_start(out=dst[s][:], in_=src[256 * s : 256 * s + 256, :].rearrange("(a p) k -> p a k", p=P))
@@ -78,26 +82,39 @@ def tile_featurepairqkscoreattribution_d2p_kernel(
                     in_=v[:, 4 * q : 4 * q + 4, :].rearrange("g q n -> q g n"),
                 )
 
-        load_pair(dk_sb, dk, 0)
+        load_one(0)
         load_scales(nc.scalar, "k", wk_scales)
+        load_one(1)
         load_words("k", wk_words)
-        load_pair(dk_sb, dk, 1)
+        load_one(2)
+        load_one(3)
         load_half(aq_sb, aq, 0)
-        load_pair(dk_sb, dk, 2)
+        load_one(4)
+        load_one(5)
         load_half(aq_sb, aq, 1)
-        load_pair(dk_sb, dk, 3)
+        load_one(6)
+        load_one(7)
+        load_half(ak_sb, ak, 0)
         load_pair(dq_sb, dq_bytes, 0)
         load_words("q", wq_words)
-        load_half(ak_sb, ak, 0)
         load_pair(dq_sb, dq_bytes, 1)
         load_half(ak_sb, ak, 1)
         load_pair(dq_sb, dq_bytes, 2)
         load_pair(dq_sb, dq_bytes, 3)
 
         make_identity(nc, ident[:])
-        load_scales(nc.gpsimd, "q", wq_scales)
-        nc.gpsimd.dma_start(out=dqs[:], in_=dq_scale.rearrange("i j -> (i j)").partition_broadcast(P))
         nc.gpsimd.dma_start(out=gt[:], in_=g.rearrange("(p t) -> p t", t=4))
+        nc.gpsimd.dma_start(out=dqs[:], in_=dq_scale.rearrange("i j -> (i j)").partition_broadcast(P))
+        load_scales(nc.gpsimd, "q", wq_scales)
+        for t in range(4):
+            nc.gpsimd.tensor_scalar(
+                out=diag[:, t, :],
+                in0=ident[:],
+                scalar1=gt[:, t : t + 1],
+                scalar2=0.0,
+                op0=MULT,
+                op1=mybir.AluOpType.add,
+            )
         nc.gpsimd.dma_start(out=hw4[:], in_=head_w.partition_broadcast(P))
         for h in range(H):
             nc.gpsimd.tensor_copy(out=hcol[32 * h : 32 * h + 32, 0:1], in_=hw4[32 * h : 32 * h + 32, h : h + 1])
@@ -122,7 +139,9 @@ def tile_featurepairqkscoreattribution_d2p_kernel(
             wide[i] = work.tile([P, D], BF16, name="wide", bufs=4)
             for j in range(8):
                 nc.vector.tensor_scalar(
-                    out=wide[i][:, P * j : P * j + P],
+                    out=wide[i][:].rearrange("p (g u m e) -> p g m u e", g=2, u=2, e=2)[
+                        :, j // 4, 32 * (j % 4) : 32 * (j % 4) + 32, :, :
+                    ],
                     in0=dq_sb[i // 2][:, i % 2, P * j : P * j + P].bitcast(FP8),
                     scalar1=dqs[:, 8 * i + j : 8 * i + j + 1],
                     scalar2=None,
@@ -130,13 +149,17 @@ def tile_featurepairqkscoreattribution_d2p_kernel(
                 )
 
         def transposes(n, i):
-            src = dk_sb[i // 2][:, i % 2, :] if n == "k" else wide[i][:]
+            src = dk_sb[i][:] if n == "k" else wide[i][:]
             words = src.bitcast(F32)
             bank = psum.tile([P, 512], F32, name="bank")
             for gg in range(2):
                 for u in range(2):
                     c = P * (2 * gg + u)
-                    nc.tensor.transpose(bank[:, c : c + P], words[:, 256 * gg + u : 256 * gg + 256 : 2], ident[:])
+                    if n == "k":
+                        w = words[:, 256 * gg + u : 256 * gg + 256 : 2]
+                    else:
+                        w = words[:, c : c + P]
+                    nc.tensor.transpose(bank[:, c : c + P], w, ident[:])
             banks[n, i] = bank
 
         def evac(n, i):
@@ -202,30 +225,26 @@ def tile_featurepairqkscoreattribution_d2p_kernel(
                 in_=il[n, h][:],
             )
 
-        gk = {}
-
-        def gmul(h):
-            gk[h] = work.tile([P, 4, 512], BF16, name="gk", bufs=2)
+        def ak_mm(x):
+            bank = psum.tile([P, 512], F32, name="bank")
+            view = bank[:].bitcast(BF16).rearrange("p (t w) -> p t w", t=4)
             for t in range(4):
-                nc.vector.tensor_scalar(
-                    out=gk[h][:, t, :], in0=ak_sb[h][:, t, :], scalar1=gt[:, t : t + 1], scalar2=None, op0=MULT
+                nc.tensor.matmul(
+                    view[:, t, :],
+                    lhsT=diag[:, t, :],
+                    rhs=ak_sb[x // 2][:, t, 256 * (x % 2) : 256 * (x % 2) + 256],
+                    start=True,
+                    stop=True,
                 )
+            banks["ak", x] = bank
 
-        fills = []
-        for h in range(2):
-            fills.append(lambda h=h: inter("aq", h, 0, aq_sb[h]))
-            fills.append(lambda h=h: inter("aq", h, 1, aq_sb[h]))
-            fills.append(lambda h=h: quant_a("aq", h))
-        for h in range(2):
-            fills.append(lambda h=h: gmul(h))
-            fills.append(lambda h=h: inter("ak", h, 0, gk[h]))
-            fills.append(lambda h=h: inter("ak", h, 1, gk[h]))
-            fills.append(lambda h=h: quant_a("ak", h))
-
-        def fill(n):
-            for x in range(min(n, len(fills))):
-                fills[0]()
-                fills.remove(fills[0])
+        def ak_empty(x):
+            if x % 2 == 0:
+                il["ak", x // 2] = work.tile([P, 2048], BF16, name="il", bufs=2, align_bytes=64)
+            nc.scalar.copy(
+                out=il["ak", x // 2][:, 1024 * (x % 2) : 1024 * (x % 2) + 1024].rearrange("p (w t) -> p w t", t=4),
+                in_=banks["ak", x][:].bitcast(BF16).rearrange("p (t w) -> p w t", t=4),
+            )
 
         const = 1.0 / (T * math.sqrt(A // H))
         otile = {}
@@ -263,7 +282,6 @@ def tile_featurepairqkscoreattribution_d2p_kernel(
         def name_tile(s, a):
             return ("k" if s < 4 else "q", 2 * (s % 4) + a)
 
-        nfill = {0: 0, 1: 3, 2: 3, 3: 3, 4: 3, 5: 2}
         for s in range(10):
             if s < 8:
                 for a in range(2):
@@ -274,19 +292,30 @@ def tile_featurepairqkscoreattribution_d2p_kernel(
                 permute("k")
             if s == 3:
                 permute("q")
+            if s in (1, 2):
+                inter("aq", s - 1, 0, aq_sb[s - 1])
             if 3 <= s < 7:
                 for a in range(2):
                     widen(2 * (s - 3) + a)
-            fill(nfill.get(s, 0))
             if s < 8:
                 for a in range(2):
                     quant1(*name_tile(s, a))
+            if s in (1, 2):
+                inter("aq", s - 1, 1, aq_sb[s - 1])
             if 1 <= s <= 8:
                 for a in range(2):
                     project(*name_tile(s - 1, a))
                 for a in range(2):
                     empty(*name_tile(s - 1, a))
+            if 2 <= s <= 5:
+                ak_mm(s - 2)
+                ak_empty(s - 2)
+            if 1 <= s <= 8:
                 quant2("k" if s - 1 < 4 else "q", (s - 1) % 4)
+            if s in (1, 2):
+                quant_a("aq", s - 1)
+            if s in (3, 5):
+                quant_a("ak", (s - 3) // 2)
             if s >= 6:
                 for a in range(2):
                     i = 2 * (s - 6) + a

@@ -44,7 +44,6 @@ def tile_featurepairqkscoreattribution_d2p_kernel(
         hw4 = keep.tile([P, 4], BF16, name="hw4")
         hcol = keep.tile([P, 1], F32, name="hcol")
         gt = keep.tile([P, 4], BF16, name="gt")
-        diag = keep.tile([P, 4, P], BF16, name="diag")
         dk_sb = [keep.tile([P, D], BF16, name="dk_sb%d" % i) for i in range(8)]
         dq_sb = [keep.tile([P, 2, D], U8, name="dq_sb%d" % s) for s in range(4)]
         aq_sb = [keep.tile([P, 4, 512], BF16, name="aq_sb%d" % s) for s in range(2)]
@@ -82,39 +81,11 @@ def tile_featurepairqkscoreattribution_d2p_kernel(
                     in_=v[:, 4 * q : 4 * q + 4, :].rearrange("g q n -> q g n"),
                 )
 
-        load_one(0)
-        load_scales(nc.scalar, "k", wk_scales)
-        load_one(1)
-        load_words("k", wk_words)
-        load_one(2)
-        load_one(3)
-        load_half(aq_sb, aq, 0)
-        load_one(4)
-        load_one(5)
-        load_half(aq_sb, aq, 1)
-        load_one(6)
-        load_one(7)
-        load_half(ak_sb, ak, 0)
-        load_pair(dq_sb, dq_bytes, 0)
-        load_words("q", wq_words)
-        load_pair(dq_sb, dq_bytes, 1)
-        load_half(ak_sb, ak, 1)
-        load_pair(dq_sb, dq_bytes, 2)
-        load_pair(dq_sb, dq_bytes, 3)
-
+        nc.scalar.dma_start(out=dqs[:], in_=dq_scale.rearrange("i j -> (i j)").partition_broadcast(P))
         make_identity(nc, ident[:])
+        load_scales(nc.gpsimd, "k", wk_scales)
         nc.gpsimd.dma_start(out=gt[:], in_=g.rearrange("(p t) -> p t", t=4))
-        nc.gpsimd.dma_start(out=dqs[:], in_=dq_scale.rearrange("i j -> (i j)").partition_broadcast(P))
         load_scales(nc.gpsimd, "q", wq_scales)
-        for t in range(4):
-            nc.gpsimd.tensor_scalar(
-                out=diag[:, t, :],
-                in0=ident[:],
-                scalar1=gt[:, t : t + 1],
-                scalar2=0.0,
-                op0=MULT,
-                op1=mybir.AluOpType.add,
-            )
         nc.gpsimd.dma_start(out=hw4[:], in_=head_w.partition_broadcast(P))
         for h in range(H):
             nc.gpsimd.tensor_copy(out=hcol[32 * h : 32 * h + 32, 0:1], in_=hw4[32 * h : 32 * h + 32, h : h + 1])
@@ -192,7 +163,7 @@ def tile_featurepairqkscoreattribution_d2p_kernel(
             banks[n, i] = bank
 
         def empty(n, i):
-            if i % 2 == 0:
+            if (n, i // 2) not in g2:
                 g2[n, i // 2] = work.tile([P, 2, 512], BF16, name="g2", bufs=3, align_bytes=64)
             dst = g2[n, i // 2][:, i % 2, :].rearrange("p (f t) -> p f t", t=4)
             src = banks[n, i][:].rearrange("p (t f) -> p f t", t=4)
@@ -210,10 +181,10 @@ def tile_featurepairqkscoreattribution_d2p_kernel(
 
         il = {}
 
-        def inter(n, h, part, src):
-            if part == 0:
-                il[n, h] = work.tile([P, 2048], BF16, name="il", bufs=2, align_bytes=64)
-            nc.vector.tensor_copy(
+        def inter(n, h, part, src, eng="v"):
+            if (n, h) not in il:
+                il[n, h] = work.tile([P, 2048], BF16, name="il", bufs=4, align_bytes=64)
+            (nc.vector.tensor_copy if eng == "v" else nc.scalar.copy)(
                 out=il[n, h][:, 1024 * part : 1024 * part + 1024].rearrange("p (w t) -> p w t", t=4),
                 in_=src[:, :, 256 * part : 256 * part + 256].rearrange("p t w -> p w t"),
             )
@@ -225,53 +196,49 @@ def tile_featurepairqkscoreattribution_d2p_kernel(
                 in_=il[n, h][:],
             )
 
-        def ak_mm(x):
-            bank = psum.tile([P, 512], F32, name="bank")
-            view = bank[:].bitcast(BF16).rearrange("p (t w) -> p t w", t=4)
-            for t in range(4):
-                nc.tensor.matmul(
-                    view[:, t, :],
-                    lhsT=diag[:, t, :],
-                    rhs=ak_sb[x // 2][:, t, 256 * (x % 2) : 256 * (x % 2) + 256],
-                    start=True,
-                    stop=True,
-                )
-            banks["ak", x] = bank
+        gk = {}
 
-        def ak_empty(x):
-            if x % 2 == 0:
-                il["ak", x // 2] = work.tile([P, 2048], BF16, name="il", bufs=2, align_bytes=64)
-            nc.scalar.copy(
-                out=il["ak", x // 2][:, 1024 * (x % 2) : 1024 * (x % 2) + 1024].rearrange("p (w t) -> p w t", t=4),
-                in_=banks["ak", x][:].bitcast(BF16).rearrange("p (t w) -> p w t", t=4),
-            )
+        def gmul(h):
+            gk[h] = work.tile([P, 4, 512], BF16, name="gk", bufs=2)
+            for t in range(4):
+                nc.vector.tensor_scalar(
+                    out=gk[h][:, t, :], in0=ak_sb[h][:, t, :], scalar1=gt[:, t : t + 1], scalar2=None, op0=MULT
+                )
 
         const = 1.0 / (T * math.sqrt(A // H))
         otile = {}
 
-        def final_mm(i, j):
-            res = []
-            for x, y in (("aq", "ak"), ("q", "k")):
-                bank = psum.tile([P, 512], F32, name="bank")
-                nc.tensor.matmul_mx(
-                    out=bank[:],
-                    lhsT=c2[x][:, P * i : P * i + P].bitcast(FP8X4),
-                    lhsT_scale=s2[x][:, P * i : P * i + P],
-                    rhs=c2[y][:, 512 * j : 512 * j + 512].bitcast(FP8X4),
-                    rhs_scale=s2[y][:, 512 * j : 512 * j + 512],
-                    start=True,
-                    stop=True,
-                )
-                res.append(bank)
-            banks["f", i, j] = res
+        def final_mm(x, y, i, j):
+            bank = psum.tile([P, 512], F32, name="bank")
+            nc.tensor.matmul_mx(
+                out=bank[:],
+                lhsT=c2[x][:, P * i : P * i + P].bitcast(FP8X4),
+                lhsT_scale=s2[x][:, P * i : P * i + P],
+                rhs=c2[y][:, 512 * j : 512 * j + 512].bitcast(FP8X4),
+                rhs_scale=s2[y][:, 512 * j : 512 * j + 512],
+                start=True,
+                stop=True,
+            )
+            banks[x, i, j] = bank
 
-        def final_ew(i, j):
-            cb, mb = banks["f", i, j]
-            cs = work.tile([P, 512], F32, name="cs", bufs=4)
-            nc.scalar.activation(out=cs[:], in_=cb[:], func=COPY, scale=const)
-            if j == 0:
+        cs = {}
+
+        def final_c(i, j):
+            final_mm("aq", "ak", i, j)
+            cs[i, j] = work.tile([P, 512], F32, name="cs", bufs=8)
+            nc.scalar.activation(out=cs[i, j][:], in_=banks["aq", i, j][:], func=COPY, scale=const)
+
+        def final_x(i, j, eng="v"):
+            final_mm("q", "k", i, j)
+            if i not in otile:
                 otile[i] = work.tile([P, 1024], F32, name="ot", bufs=4)
-            nc.vector.tensor_tensor(out=otile[i][:, 512 * j : 512 * j + 512], in0=mb[:], in1=cs[:], op=MULT)
+            dst = otile[i][:, 512 * j : 512 * j + 512]
+            if eng == "v":
+                nc.vector.tensor_tensor(out=dst, in0=banks["q", i, j][:], in1=cs[i, j][:], op=MULT)
+            else:
+                ms = work.tile([P, 512], F32, name="ms", bufs=3)
+                nc.scalar.copy(out=ms[:], in_=banks["q", i, j][:])
+                nc.gpsimd.tensor_tensor(out=dst, in0=ms[:], in1=cs[i, j][:], op=MULT)
             if i == 7:
                 nc.sync.dma_start(
                     out=out[P * i : P * i + P, 512 * j : 512 * j + 512], in_=otile[i][:, 512 * j : 512 * j + 512]
@@ -282,43 +249,37 @@ def tile_featurepairqkscoreattribution_d2p_kernel(
         def name_tile(s, a):
             return ("k" if s < 4 else "q", 2 * (s % 4) + a)
 
-        for s in range(10):
-            if s < 8:
-                for a in range(2):
-                    transposes(*name_tile(s, a))
-                for a in range(2):
-                    evac(*name_tile(s, a))
-            if s == 0:
-                permute("k")
-            if s == 3:
-                permute("q")
-            if s in (1, 2):
-                inter("aq", s - 1, 0, aq_sb[s - 1])
-            if 3 <= s < 7:
-                for a in range(2):
-                    widen(2 * (s - 3) + a)
-            if s < 8:
-                for a in range(2):
-                    quant1(*name_tile(s, a))
-            if s in (1, 2):
-                inter("aq", s - 1, 1, aq_sb[s - 1])
-            if 1 <= s <= 8:
-                for a in range(2):
-                    project(*name_tile(s - 1, a))
-                for a in range(2):
-                    empty(*name_tile(s - 1, a))
-            if 2 <= s <= 5:
-                ak_mm(s - 2)
-                ak_empty(s - 2)
-            if 1 <= s <= 8:
-                quant2("k" if s - 1 < 4 else "q", (s - 1) % 4)
-            if s in (1, 2):
-                quant_a("aq", s - 1)
-            if s in (3, 5):
-                quant_a("ak", (s - 3) // 2)
-            if s >= 6:
-                for a in range(2):
-                    i = 2 * (s - 6) + a
-                    for j in range(2):
-                        final_mm(i, j)
-                        final_ew(i, j)
+        def tile_of(n):
+            return ("k" if n < 8 else "q", n % 8)
+
+        run = {
+            "T": lambda n: transposes(*tile_of(n)),
+            "E": lambda n: evac(*tile_of(n)),
+            "Q": lambda n: quant1(*tile_of(n)),
+            "M": lambda n: project(*tile_of(n)),
+            "P": lambda n: empty(*tile_of(n)),
+            "D": lambda i: load_one(i),
+            "d": lambda s: load_pair(dq_sb, dq_bytes, s),
+            "a": lambda s: load_half(aq_sb, aq, s),
+            "b": lambda s: load_half(ak_sb, ak, s),
+            "w": lambda s: load_words("kq"[s], (wk_words, wq_words)[s]),
+            "R": lambda s: quant2("k" if s < 4 else "q", s % 4),
+            "W": lambda i: widen(i),
+            "k": lambda s: permute("k"),
+            "q": lambda s: permute("q"),
+            "i": lambda s: inter("aq", s // 2, s % 2, aq_sb[s // 2]),
+            "I": lambda s: inter("aq", s // 2, s % 2, aq_sb[s // 2], "s"),
+            "j": lambda s: inter("ak", s // 2, s % 2, gk[s // 2]),
+            "J": lambda s: inter("ak", s // 2, s % 2, gk[s // 2], "s"),
+            "g": lambda s: gmul(s),
+            "x": lambda s: quant_a("aq", s),
+            "y": lambda s: quant_a("ak", s),
+            "C": lambda s: final_c(s // 2, s % 2),
+            "X": lambda s: final_x(s // 2, s % 2),
+            "Z": lambda s: final_x(s // 2, s % 2, "g"),
+        }
+        order = """
+            D0 D1 w0 D2 D3 d0 a0 D4 D5 w1 d1 D6 D7 a1 d2 b0 d3 b1 T0 T1 E0 E1 Q0 Q1 W0 W1 i0 T2 T3 E2 E3 k0 Q2 Q3 i1 T8 T9 E8 E9 Q8 Q9 W2 W3 x0 T4 T5 E4 E5 q0 Q4 Q5 W4 W5 M0 M1 P0 P1 g0 T6 T7 E6 E7 Q6 Q7 W6 W7 M2 M3 P2 P3 j0 R0 T10 T11 E10 E11 Q10 Q11 M8 M9 P8 P9 J1 R1 T12 T13 E12 E13 Q12 Q13 M4 M5 P4 P5 y0 R4 T14 T15 E14 E15 Q14 Q15 M6 M7 P6 P7 g1 R2 M10 M11 P10 P11 j2 R3 M12 M13 P12 P13 j3 R5 M14 M15 P14 P15 y1 R6 I2 R7 i3 x1 C0 C1 X0 C2 X1 C3 X2 C4 X3 C5 X4 C6 X5 C7 X6 C8 X7 C9 X8 C10 X9 C11 X10 C12 X11 C13 X12 C14 X13 C15 X14 X15
+        """
+        for token in order.split():
+            run[token[0]](int(token[1:]))

@@ -81,14 +81,18 @@ def tile_featurepairqkscoreattribution_d2p_kernel(
                     in_=v[:, 4 * q : 4 * q + 4, :].rearrange("g q n -> q g n"),
                 )
 
-        nc.scalar.dma_start(out=dqs[:], in_=dq_scale.rearrange("i j -> (i j)").partition_broadcast(P))
         make_identity(nc, ident[:])
-        load_scales(nc.gpsimd, "k", wk_scales)
-        nc.gpsimd.dma_start(out=gt[:], in_=g.rearrange("(p t) -> p t", t=4))
-        load_scales(nc.gpsimd, "q", wq_scales)
-        nc.gpsimd.dma_start(out=hw4[:], in_=head_w.partition_broadcast(P))
-        for h in range(H):
-            nc.gpsimd.tensor_copy(out=hcol[32 * h : 32 * h + 32, 0:1], in_=hw4[32 * h : 32 * h + 32, h : h + 1])
+
+        def load_small():
+            nc.sync.dma_start(out=gt[:], in_=g.rearrange("(p t) -> p t", t=4))
+            nc.sync.dma_start(out=hw4[:], in_=head_w.partition_broadcast(P))
+
+        def head_columns():
+            for h in range(H):
+                nc.scalar.copy(out=hcol[32 * h : 32 * h + 32, 0:1], in_=hw4[32 * h : 32 * h + 32, h : h + 1])
+
+        def load_dqs():
+            nc.scalar.dma_start(out=dqs[:], in_=dq_scale.rearrange("i j -> (i j)").partition_broadcast(P))
 
         def permute(n):
             nc.vector.tensor_copy(
@@ -107,7 +111,7 @@ def tile_featurepairqkscoreattribution_d2p_kernel(
         g2 = {}
 
         def widen(i):
-            wide[i] = work.tile([P, D], BF16, name="wide", bufs=4)
+            wide[i] = work.tile([P, D], BF16, name="wide", bufs=8)
             for j in range(8):
                 nc.vector.tensor_scalar(
                     out=wide[i][:].rearrange("p (g u m e) -> p g m u e", g=2, u=2, e=2)[
@@ -134,15 +138,15 @@ def tile_featurepairqkscoreattribution_d2p_kernel(
             banks[n, i] = bank
 
         def evac(n, i):
-            kt[n, i] = work.tile([P, 1024], BF16, name="kt", bufs=4, align_bytes=64)
+            kt[n, i] = work.tile([P, 1024], BF16, name="kt", bufs=8, align_bytes=64)
             nc.scalar.copy(
                 out=kt[n, i][:].bitcast(F32).rearrange("p (g f u) -> p g f u", g=2, u=2),
                 in_=banks[n, i][:].rearrange("p (g u f) -> p g f u", g=2, u=2),
             )
 
         def quant1(n, i):
-            cc = work.tile([P, 256], U32, name="c1", bufs=6, align_bytes=64)
-            ss = work.tile([P, 256], U8, name="s1", bufs=6, align_bytes=64)
+            cc = work.tile([P, 256], U32, name="c1", bufs=12, align_bytes=64)
+            ss = work.tile([P, 256], U8, name="s1", bufs=12, align_bytes=64)
             nc.vector.quantize_mx(out=cc[:].bitcast(FP8X4), scales=ss[:], in_=kt[n, i][:])
             c1[n, i] = (cc, ss)
 
@@ -164,7 +168,7 @@ def tile_featurepairqkscoreattribution_d2p_kernel(
 
         def empty(n, i):
             if (n, i // 2) not in g2:
-                g2[n, i // 2] = work.tile([P, 2, 512], BF16, name="g2", bufs=3, align_bytes=64)
+                g2[n, i // 2] = work.tile([P, 2, 512], BF16, name="g2", bufs=4, align_bytes=64)
             dst = g2[n, i // 2][:, i % 2, :].rearrange("p (f t) -> p f t", t=4)
             src = banks[n, i][:].rearrange("p (t f) -> p f t", t=4)
             if n == "k":
@@ -185,8 +189,8 @@ def tile_featurepairqkscoreattribution_d2p_kernel(
             if (n, h) not in il:
                 il[n, h] = work.tile([P, 2048], BF16, name="il", bufs=4, align_bytes=64)
             (nc.vector.tensor_copy if eng == "v" else nc.scalar.copy)(
-                out=il[n, h][:, 1024 * part : 1024 * part + 1024].rearrange("p (w t) -> p w t", t=4),
-                in_=src[:, :, 256 * part : 256 * part + 256].rearrange("p t w -> p w t"),
+                out=il[n, h][:, 1024 * part : 1024 * part + 1024].rearrange("p (c i t) -> p c t i", i=4, t=4),
+                in_=src[:, :, 256 * part : 256 * part + 256].rearrange("p t (c i) -> p c t i", i=4),
             )
 
         def quant_a(n, h):
@@ -206,7 +210,6 @@ def tile_featurepairqkscoreattribution_d2p_kernel(
                 )
 
         const = 1.0 / (T * math.sqrt(A // H))
-        otile = {}
 
         def final_mm(x, y, i, j):
             bank = psum.tile([P, 512], F32, name="bank")
@@ -230,21 +233,14 @@ def tile_featurepairqkscoreattribution_d2p_kernel(
 
         def final_x(i, j, eng="v"):
             final_mm("q", "k", i, j)
-            if i not in otile:
-                otile[i] = work.tile([P, 1024], F32, name="ot", bufs=4)
-            dst = otile[i][:, 512 * j : 512 * j + 512]
+            ot = work.tile([P, 512], F32, name="ot", bufs=8)
             if eng == "v":
-                nc.vector.tensor_tensor(out=dst, in0=banks["q", i, j][:], in1=cs[i, j][:], op=MULT)
+                nc.vector.tensor_tensor(out=ot[:], in0=banks["q", i, j][:], in1=cs[i, j][:], op=MULT)
             else:
                 ms = work.tile([P, 512], F32, name="ms", bufs=3)
                 nc.scalar.copy(out=ms[:], in_=banks["q", i, j][:])
-                nc.gpsimd.tensor_tensor(out=dst, in0=ms[:], in1=cs[i, j][:], op=MULT)
-            if i == 7:
-                nc.sync.dma_start(
-                    out=out[P * i : P * i + P, 512 * j : 512 * j + 512], in_=otile[i][:, 512 * j : 512 * j + 512]
-                )
-            elif j == 1:
-                nc.sync.dma_start(out=out[P * i : P * i + P, :], in_=otile[i][:])
+                nc.gpsimd.tensor_tensor(out=ot[:], in0=ms[:], in1=cs[i, j][:], op=MULT)
+            nc.sync.dma_start(out=out[P * i : P * i + P, 512 * j : 512 * j + 512], in_=ot[:])
 
         def name_tile(s, a):
             return ("k" if s < 4 else "q", 2 * (s % 4) + a)
@@ -265,6 +261,10 @@ def tile_featurepairqkscoreattribution_d2p_kernel(
             "w": lambda s: load_words("kq"[s], (wk_words, wq_words)[s]),
             "R": lambda s: quant2("k" if s < 4 else "q", s % 4),
             "W": lambda i: widen(i),
+            "u": lambda s: load_dqs(),
+            "s": lambda s: load_scales((nc.scalar, nc.sync)[s], "kq"[s], (wk_scales, wq_scales)[s]),
+            "v": lambda s: load_small(),
+            "h": lambda s: head_columns(),
             "k": lambda s: permute("k"),
             "q": lambda s: permute("q"),
             "i": lambda s: inter("aq", s // 2, s % 2, aq_sb[s // 2]),
@@ -279,7 +279,7 @@ def tile_featurepairqkscoreattribution_d2p_kernel(
             "Z": lambda s: final_x(s // 2, s % 2, "g"),
         }
         order = """
-            D0 D1 w0 D2 D3 d0 a0 D4 D5 w1 d1 D6 D7 a1 d2 b0 d3 b1 T0 T1 E0 E1 Q0 Q1 W0 W1 i0 T2 T3 E2 E3 k0 Q2 Q3 i1 T8 T9 E8 E9 Q8 Q9 W2 W3 x0 T4 T5 E4 E5 q0 Q4 Q5 W4 W5 M0 M1 P0 P1 g0 T6 T7 E6 E7 Q6 Q7 W6 W7 M2 M3 P2 P3 j0 R0 T10 T11 E10 E11 Q10 Q11 M8 M9 P8 P9 J1 R1 T12 T13 E12 E13 Q12 Q13 M4 M5 P4 P5 y0 R4 T14 T15 E14 E15 Q14 Q15 M6 M7 P6 P7 g1 R2 M10 M11 P10 P11 j2 R3 M12 M13 P12 P13 j3 R5 M14 M15 P14 P15 y1 R6 I2 R7 i3 x1 C0 C1 X0 C2 X1 C3 X2 C4 X3 C5 X4 C6 X5 C7 X6 C8 X7 C9 X8 C10 X9 C11 X10 C12 X11 C13 X12 C14 X13 C15 X14 X15
+            D0 D1 u0 s0 d0 w0 D2 D3 d1 w1 a0 D4 s1 v0 D5 d2 b0 D6 D7 d3 a1 b1 T0 T1 E0 E1 W0 W1 T8 T9 E8 E9 k0 Q0 Q1 T2 T3 E2 E3 W2 W3 q0 Q8 Q9 M0 M1 P0 P1 I0 T10 T11 E10 E11 i1 Q2 Q3 h0 M8 M9 P8 P9 x0 R0 T4 T5 E4 E5 W4 W5 g0 Q10 Q11 M2 M3 P2 P3 j0 R4 T12 T13 E12 E13 j1 Q4 Q5 M10 M11 P10 P11 y0 R1 T6 T7 E6 E7 W6 W7 Q12 Q13 C0 M4 M5 P4 P5 I2 R5 T14 T15 E14 E15 i3 Q6 Q7 C2 X0 M12 M13 P12 P13 x1 R2 g1 Q14 Q15 C4 X2 M6 M7 P6 P7 j2 R6 j3 C6 X4 M14 M15 P14 P15 y1 R3 C8 X6 R7 C10 X8 C12 X10 C14 X12 C1 X14 C3 X1 C5 X3 C7 X5 C9 X7 C11 X9 C13 X11 C15 X13 X15
         """
         for token in order.split():
             run[token[0]](int(token[1:]))

@@ -4,8 +4,12 @@ from contextlib import ExitStack
 import concourse.mybir as mybir
 from concourse.masks import make_identity
 
-F, J, D, A, H, T = 1024, 1024, 1024, 512, 4, 512
-FLOPS = 2 * (2 * 1024 * D * A + F * J * A + F * J * T)
+N_FEAT = 1024
+WIDTH = 1024
+CHANNELS = 512
+HEADS = 4
+TOKENS = 512
+FLOPS = 2 * N_FEAT * (2 * WIDTH * CHANNELS + N_FEAT * CHANNELS + N_FEAT * TOKENS)
 
 F32 = mybir.dt.float32
 BF16 = mybir.dt.bfloat16
@@ -17,7 +21,14 @@ FP8X4 = mybir.dt.float8_e4m3fn_x4
 FP4X4 = mybir.dt.float4_e2m1fn_x4
 MULT = mybir.AluOpType.mult
 COPY = mybir.ActivationFunctionType.Copy
+
 P = 128
+PACK = 4
+HALF = 512
+TILES = N_FEAT // P
+CHAIN = [(side, pair) for pair in range(TILES // 2) for side in ("k", "q")]
+PIECES = [(i, j) for j in range(2) for i in range(TILES)]
+FIRST_PIECE_STEP = 6
 
 
 def tile_featurepairqkscoreattribution_d2p_kernel(
@@ -31,255 +42,270 @@ def tile_featurepairqkscoreattribution_d2p_kernel(
         ctx.enter_context(tc.manual_schedule())
 
         ident = keep.tile([P, P], F32, name="ident")
-        sc_raw = {}
-        sc = {}
-        wd_raw = {}
-        wd = {}
-        for n in ("k", "q"):
-            sc_raw[n] = keep.tile([P, 256], I32, name="sc_raw_" + n, align_bytes=64)
-            sc[n] = keep.tile([P, 256], I32, name="sc_" + n, align_bytes=64)
-            wd_raw[n] = keep.tile([P, 512], I32, name="wd_raw_" + n, align_bytes=64)
-            wd[n] = keep.tile([P, 512], I32, name="wd_" + n, align_bytes=64)
-        dqs = keep.tile([P, 64], F32, name="dqs")
-        hw4 = keep.tile([P, 4], BF16, name="hw4")
-        hcol = keep.tile([P, 1], F32, name="hcol")
-        gt = keep.tile([P, 4], BF16, name="gt")
-        dk_sb = [keep.tile([P, D], BF16, name="dk_sb%d" % i) for i in range(8)]
-        dq_sb = [keep.tile([P, 2, D], U8, name="dq_sb%d" % s) for s in range(4)]
-        aq_sb = [keep.tile([P, 4, 512], BF16, name="aq_sb%d" % s) for s in range(2)]
-        ak_sb = [keep.tile([P, 4, 512], BF16, name="ak_sb%d" % s) for s in range(2)]
-        c2 = {}
-        s2 = {}
-        for n in ("k", "q", "aq", "ak"):
-            c2[n] = keep.tile([P, 1024], U32, name="c2_" + n, align_bytes=64)
-            s2[n] = keep.tile([P, 1024], U8, name="s2_" + n, align_bytes=64)
+        dk_in = [keep.tile([P, WIDTH], BF16, name="dk_in%d" % i) for i in range(TILES)]
+        dq_in = [keep.tile([P, 2, WIDTH], U8, name="dq_in%d" % s) for s in range(TILES // 2)]
+        dq_sc = keep.tile([P, 64], F32, name="dq_sc")
+        aq_in = [keep.tile([P, PACK, HALF], BF16, name="aq_in%d" % h) for h in range(2)]
+        ak_in = [keep.tile([P, PACK, HALF], BF16, name="ak_in%d" % h) for h in range(2)]
+        g_in = keep.tile([P, PACK], BF16, name="g_in")
+        head_in = keep.tile([P, HEADS], BF16, name="head_in")
+        head_col = keep.tile([P, 1], F32, name="head_col")
+        words_in, words, scales_in, scales = {}, {}, {}, {}
+        for side in ("k", "q"):
+            words_in[side] = keep.tile([P, 512], I32, name="words_in_" + side, align_bytes=64)
+            words[side] = keep.tile([P, 512], I32, name="words_" + side, align_bytes=64)
+            scales_in[side] = keep.tile([P, 256], I32, name="scales_in_" + side, align_bytes=64)
+            scales[side] = keep.tile([P, 256], I32, name="scales_" + side, align_bytes=64)
+        codes2, scales2 = {}, {}
+        for name in ("k", "q", "aq", "ak"):
+            codes2[name] = keep.tile([P, N_FEAT], U32, name="codes2_" + name, align_bytes=64)
+            scales2[name] = keep.tile([P, N_FEAT], U8, name="scales2_" + name, align_bytes=64)
 
-        nc.vector.memset(sc_raw["k"][:], 0)
-        nc.vector.memset(sc_raw["q"][:], 0)
-
-        def load_one(i):
-            nc.sync.dma_start(out=dk_sb[i][:], in_=dk[P * i : P * i + P, :])
-
-        def load_pair(dst, src, s):
-            nc.sync.dma_start(out=dst[s][:], in_=src[256 * s : 256 * s + 256, :].rearrange("(a p) k -> p a k", p=P))
-
-        def load_half(dst, src, h):
-            nc.sync.dma_start(
-                out=dst[h][:], in_=src[:, 512 * h : 512 * h + 512].rearrange("(p t) w -> p t w", t=4)
-            )
-
-        def load_words(n, src):
-            nc.sync.dma_start(
-                out=wd_raw[n][:].rearrange("p (g n) -> p g n", g=2), in_=src.bitcast(I32).rearrange("g p n -> p g n")
-            )
-
-        def load_scales(eng, n, src):
-            v = src.bitcast(I32)
-            for q in range(4):
-                eng.dma_start(
-                    out=sc_raw[n][32 * q : 32 * q + 4, :].rearrange("q (g n) -> q g n", g=2),
-                    in_=v[:, 4 * q : 4 * q + 4, :].rearrange("g q n -> q g n"),
-                )
-
+        for side in ("k", "q"):
+            nc.vector.memset(scales_in[side][:], 0)
         make_identity(nc, ident[:])
 
-        def load_small():
-            nc.sync.dma_start(out=gt[:], in_=g.rearrange("(p t) -> p t", t=4))
-            nc.sync.dma_start(out=hw4[:], in_=head_w.partition_broadcast(P))
+        def load_dk(i):
+            nc.sync.dma_start(out=dk_in[i][:], in_=dk[P * i : P * i + P, :])
 
-        def head_columns():
-            for h in range(H):
-                nc.scalar.copy(out=hcol[32 * h : 32 * h + 32, 0:1], in_=hw4[32 * h : 32 * h + 32, h : h + 1])
+        def load_dq(s):
+            rows = dq_bytes[2 * P * s : 2 * P * s + 2 * P, :]
+            nc.sync.dma_start(out=dq_in[s][:], in_=rows.rearrange("(a p) k -> p a k", p=P))
 
-        def load_dqs():
-            nc.scalar.dma_start(out=dqs[:], in_=dq_scale.rearrange("i j -> (i j)").partition_broadcast(P))
+        def load_tokens(dst, src, h):
+            cols = src[:, HALF * h : HALF * h + HALF]
+            nc.sync.dma_start(out=dst[h][:], in_=cols.rearrange("(p t) w -> p t w", t=PACK))
 
-        def permute(n):
-            nc.vector.tensor_copy(
-                out=wd[n][:].rearrange("p (t b w) -> p t b w", t=4, w=4),
-                in_=wd_raw[n][:].rearrange("p (b t w) -> p t b w", t=4, w=4),
-            )
-            nc.vector.tensor_copy(
-                out=sc[n][:].rearrange("p (t b w) -> p t b w", t=4, w=2),
-                in_=sc_raw[n][:].rearrange("p (b t w) -> p t b w", t=4, w=2),
+        def load_words(side, src):
+            nc.sync.dma_start(
+                out=words_in[side][:].rearrange("p (g n) -> p g n", g=2),
+                in_=src.bitcast(I32).rearrange("g p n -> p g n"),
             )
 
-        wide = {}
-        banks = {}
-        kt = {}
-        c1 = {}
-        g2 = {}
+        def load_scales(queue, side, src):
+            rows = src.bitcast(I32)
+            for quad in range(4):
+                queue.dma_start(
+                    out=scales_in[side][32 * quad : 32 * quad + 4, :].rearrange("r (g n) -> r g n", g=2),
+                    in_=rows[:, 4 * quad : 4 * quad + 4, :].rearrange("g r n -> r g n"),
+                )
+
+        load_dk(0)
+        load_dq(0)
+        nc.scalar.dma_start(out=dq_sc[:], in_=dq_scale.rearrange("i j -> (i j)").partition_broadcast(P))
+        load_dk(1)
+        load_scales(nc.scalar, "k", wk_scales)
+        load_words("k", wk_words)
+        load_dk(2)
+        load_dk(3)
+        load_dq(1)
+        load_words("q", wq_words)
+        load_scales(nc.sync, "q", wq_scales)
+        load_tokens(aq_in, aq, 0)
+        load_dk(4)
+        nc.sync.dma_start(out=g_in[:], in_=g.rearrange("(p t) -> p t", t=PACK))
+        nc.sync.dma_start(out=head_in[:], in_=head_w.partition_broadcast(P))
+        load_dk(5)
+        load_dq(2)
+        load_tokens(ak_in, ak, 0)
+        load_dk(6)
+        load_dk(7)
+        load_dq(3)
+        load_tokens(aq_in, aq, 1)
+        load_tokens(ak_in, ak, 1)
+
+        def order_channels(side):
+            for dst, src, run in ((words, words_in, 4), (scales, scales_in, 2)):
+                nc.vector.tensor_copy(
+                    out=dst[side][:].rearrange("p (t x w) -> p t x w", t=4, w=run),
+                    in_=src[side][:].rearrange("p (x t w) -> p t x w", t=4, w=run),
+                )
+
+        def spread_heads():
+            for h in range(HEADS):
+                rows = slice(32 * h, 32 * h + 32)
+                nc.scalar.copy(out=head_col[rows, 0:1], in_=head_in[rows, h : h + 1])
+
+        dq_wide, first_in, first_q, second_in, bank_of = {}, {}, {}, {}, {}
 
         def widen(i):
-            wide[i] = work.tile([P, D], BF16, name="wide", bufs=8)
+            dq_wide[i] = work.tile([P, WIDTH], BF16, name="wide", bufs=8)
+            by_pass = dq_wide[i][:].rearrange("p (g u m e) -> p g m u e", g=2, u=2, e=2)
             for j in range(8):
                 nc.vector.tensor_scalar(
-                    out=wide[i][:].rearrange("p (g u m e) -> p g m u e", g=2, u=2, e=2)[
-                        :, j // 4, 32 * (j % 4) : 32 * (j % 4) + 32, :, :
-                    ],
-                    in0=dq_sb[i // 2][:, i % 2, P * j : P * j + P].bitcast(FP8),
-                    scalar1=dqs[:, 8 * i + j : 8 * i + j + 1],
+                    out=by_pass[:, j // 4, 32 * (j % 4) : 32 * (j % 4) + 32, :, :],
+                    in0=dq_in[i // 2][:, i % 2, P * j : P * j + P].bitcast(FP8),
+                    scalar1=dq_sc[:, 8 * i + j : 8 * i + j + 1],
                     scalar2=None,
                     op0=MULT,
                 )
 
-        def transposes(n, i):
-            src = dk_sb[i][:] if n == "k" else wide[i][:]
-            words = src.bitcast(F32)
-            bank = psum.tile([P, 512], F32, name="bank")
+        def transpose(side, i):
+            pairs = (dk_in[i] if side == "k" else dq_wide[i])[:].bitcast(F32)
+            bank = psum.tile([P, HALF], F32, name="bank")
             for gg in range(2):
                 for u in range(2):
-                    c = P * (2 * gg + u)
-                    if n == "k":
-                        w = words[:, 256 * gg + u : 256 * gg + 256 : 2]
+                    at = P * (2 * gg + u)
+                    if side == "k":
+                        src = pairs[:, 2 * P * gg + u : 2 * P * gg + 2 * P : 2]
                     else:
-                        w = words[:, c : c + P]
-                    nc.tensor.transpose(bank[:, c : c + P], w, ident[:])
-            banks[n, i] = bank
+                        src = pairs[:, at : at + P]
+                    nc.tensor.transpose(bank[:, at : at + P], src, ident[:])
+            bank_of[side, i] = bank
 
-        def evac(n, i):
-            kt[n, i] = work.tile([P, 1024], BF16, name="kt", bufs=8, align_bytes=64)
+        def collect(side, i):
+            if (side, i // 2) not in first_in:
+                first_in[side, i // 2] = work.tile([P, 2048], BF16, name="first_in", bufs=4, align_bytes=64)
+            dst = first_in[side, i // 2][:, 1024 * (i % 2) : 1024 * (i % 2) + 1024]
             nc.scalar.copy(
-                out=kt[n, i][:].bitcast(F32).rearrange("p (g f u) -> p g f u", g=2, u=2),
-                in_=banks[n, i][:].rearrange("p (g u f) -> p g f u", g=2, u=2),
+                out=dst.bitcast(F32).rearrange("p (g f u) -> p g f u", g=2, u=2),
+                in_=bank_of[side, i][:].rearrange("p (g u f) -> p g f u", g=2, u=2),
             )
 
-        def quant1(n, i):
-            cc = work.tile([P, 256], U32, name="c1", bufs=12, align_bytes=64)
-            ss = work.tile([P, 256], U8, name="s1", bufs=12, align_bytes=64)
-            nc.vector.quantize_mx(out=cc[:].bitcast(FP8X4), scales=ss[:], in_=kt[n, i][:])
-            c1[n, i] = (cc, ss)
+        def quantize_first(side, s):
+            codes = work.tile([P, 512], U32, name="codes1", bufs=6, align_bytes=64)
+            sc = work.tile([P, 512], U8, name="scales1", bufs=6, align_bytes=64)
+            nc.vector.quantize_mx(out=codes[:].bitcast(FP8X4), scales=sc[:], in_=first_in[side, s][:])
+            first_q[side, s] = (codes, sc)
 
-        def project(n, i):
-            cc, ss = c1[n, i]
-            bank = psum.tile([P, 512], F32, name="bank")
-            for t in range(4):
+        def project(side, i):
+            codes, sc = first_q[side, i // 2]
+            bank = psum.tile([P, HALF], F32, name="bank")
+            for t in range(PACK):
                 for gg in range(2):
+                    at = P * (2 * (i % 2) + gg)
                     nc.tensor.matmul_mx(
                         out=bank[:, P * t : P * t + P],
-                        lhsT=wd[n][:, 128 * t + 64 * gg : 128 * t + 64 * gg + 64].bitcast(FP4X4),
-                        lhsT_scale=sc[n][:, 64 * t + 32 * gg : 64 * t + 32 * gg + 32].bitcast(U8),
-                        rhs=cc[:, P * gg : P * gg + P].bitcast(FP8X4),
-                        rhs_scale=ss[:, P * gg : P * gg + P],
+                        lhsT=words[side][:, 128 * t + 64 * gg : 128 * t + 64 * gg + 64].bitcast(FP4X4),
+                        lhsT_scale=scales[side][:, 64 * t + 32 * gg : 64 * t + 32 * gg + 32].bitcast(U8),
+                        rhs=codes[:, at : at + P].bitcast(FP8X4),
+                        rhs_scale=sc[:, at : at + P],
                         start=(gg == 0),
                         stop=(gg == 1),
                     )
-            banks[n, i] = bank
+            bank_of[side, i] = bank
 
-        def empty(n, i):
-            if (n, i // 2) not in g2:
-                g2[n, i // 2] = work.tile([P, 2, 512], BF16, name="g2", bufs=4, align_bytes=64)
-            dst = g2[n, i // 2][:, i % 2, :].rearrange("p (f t) -> p f t", t=4)
-            src = banks[n, i][:].rearrange("p (t f) -> p f t", t=4)
-            if n == "k":
+        def round_projection(side, i):
+            if (side, i // 2) not in second_in:
+                second_in[side, i // 2] = work.tile([P, 2, HALF], BF16, name="second_in", bufs=4, align_bytes=64)
+            dst = second_in[side, i // 2][:, i % 2, :].rearrange("p (f t) -> p f t", t=PACK)
+            src = bank_of[side, i][:].rearrange("p (t f) -> p f t", t=PACK)
+            if side == "k":
                 nc.scalar.copy(out=dst, in_=src)
             else:
-                nc.scalar.activation(out=dst, in_=src, func=COPY, scale=hcol[:, 0:1])
+                nc.scalar.activation(out=dst, in_=src, func=COPY, scale=head_col[:, 0:1])
 
-        def quant2(n, s):
+        def quantize_second(side, s):
+            cols = slice(2 * P * s, 2 * P * s + 2 * P)
             nc.vector.quantize_mx(
-                out=c2[n][:, 256 * s : 256 * s + 256].bitcast(FP8X4),
-                scales=s2[n][:, 256 * s : 256 * s + 256],
-                in_=g2[n, s][:].rearrange("p a c -> p (a c)"),
+                out=codes2[side][:, cols].bitcast(FP8X4),
+                scales=scales2[side][:, cols],
+                in_=second_in[side, s][:].rearrange("p a c -> p (a c)"),
             )
 
-        il = {}
+        ak_g, side_by_side = {}, {}
 
-        def inter(n, h, part, src, eng="v"):
-            if (n, h) not in il:
-                il[n, h] = work.tile([P, 2048], BF16, name="il", bufs=4, align_bytes=64)
-            (nc.vector.tensor_copy if eng == "v" else nc.scalar.copy)(
-                out=il[n, h][:, 1024 * part : 1024 * part + 1024].rearrange("p (c i t) -> p c t i", i=4, t=4),
+        def multiply_g(h):
+            ak_g[h] = work.tile([P, PACK, HALF], BF16, name="ak_g", bufs=2)
+            for t in range(PACK):
+                nc.vector.tensor_scalar(
+                    out=ak_g[h][:, t, :], in0=ak_in[h][:, t, :], scalar1=g_in[:, t : t + 1], scalar2=None, op0=MULT
+                )
+
+        def interleave(name, h, part, copy):
+            if (name, h) not in side_by_side:
+                side_by_side[name, h] = work.tile([P, 2048], BF16, name="side_by_side", bufs=4, align_bytes=64)
+            src = aq_in[h] if name == "aq" else ak_g[h]
+            copy(
+                out=side_by_side[name, h][:, 1024 * part : 1024 * part + 1024].rearrange(
+                    "p (c i t) -> p c t i", i=4, t=PACK
+                ),
                 in_=src[:, :, 256 * part : 256 * part + 256].rearrange("p t (c i) -> p c t i", i=4),
             )
 
-        def quant_a(n, h):
+        def quantize_tokens(name, h):
+            cols = slice(HALF * h, HALF * h + HALF)
             nc.vector.quantize_mx(
-                out=c2[n][:, 512 * h : 512 * h + 512].bitcast(FP8X4),
-                scales=s2[n][:, 512 * h : 512 * h + 512],
-                in_=il[n, h][:],
+                out=codes2[name][:, cols].bitcast(FP8X4), scales=scales2[name][:, cols], in_=side_by_side[name, h][:]
             )
 
-        gk = {}
+        divisor = 1.0 / (TOKENS * math.sqrt(CHANNELS // HEADS))
+        c_part = {}
 
-        def gmul(h):
-            gk[h] = work.tile([P, 4, 512], BF16, name="gk", bufs=2)
-            for t in range(4):
-                nc.vector.tensor_scalar(
-                    out=gk[h][:, t, :], in0=ak_sb[h][:, t, :], scalar1=gt[:, t : t + 1], scalar2=None, op0=MULT
-                )
-
-        const = 1.0 / (T * math.sqrt(A // H))
-
-        def final_mm(x, y, i, j):
-            bank = psum.tile([P, 512], F32, name="bank")
+        def product(rows, cols, i, j):
+            bank = psum.tile([P, HALF], F32, name="bank")
             nc.tensor.matmul_mx(
                 out=bank[:],
-                lhsT=c2[x][:, P * i : P * i + P].bitcast(FP8X4),
-                lhsT_scale=s2[x][:, P * i : P * i + P],
-                rhs=c2[y][:, 512 * j : 512 * j + 512].bitcast(FP8X4),
-                rhs_scale=s2[y][:, 512 * j : 512 * j + 512],
+                lhsT=codes2[rows][:, P * i : P * i + P].bitcast(FP8X4),
+                lhsT_scale=scales2[rows][:, P * i : P * i + P],
+                rhs=codes2[cols][:, HALF * j : HALF * j + HALF].bitcast(FP8X4),
+                rhs_scale=scales2[cols][:, HALF * j : HALF * j + HALF],
                 start=True,
                 stop=True,
             )
-            banks[x, i, j] = bank
+            return bank
 
-        cs = {}
+        def begin_piece(i, j):
+            bank = product("aq", "ak", i, j)
+            c_part[i, j] = work.tile([P, HALF], F32, name="c_part", bufs=8)
+            nc.scalar.activation(out=c_part[i, j][:], in_=bank[:], func=COPY, scale=divisor)
 
-        def final_c(i, j):
-            final_mm("aq", "ak", i, j)
-            cs[i, j] = work.tile([P, 512], F32, name="cs", bufs=8)
-            nc.scalar.activation(out=cs[i, j][:], in_=banks["aq", i, j][:], func=COPY, scale=const)
+        def finish_piece(i, j):
+            bank = product("q", "k", i, j)
+            piece = work.tile([P, HALF], F32, name="piece", bufs=8)
+            nc.vector.tensor_tensor(out=piece[:], in0=bank[:], in1=c_part[i, j][:], op=MULT)
+            nc.sync.dma_start(out=out[P * i : P * i + P, HALF * j : HALF * j + HALF], in_=piece[:])
 
-        def final_x(i, j, eng="v"):
-            final_mm("q", "k", i, j)
-            ot = work.tile([P, 512], F32, name="ot", bufs=8)
-            if eng == "v":
-                nc.vector.tensor_tensor(out=ot[:], in0=banks["q", i, j][:], in1=cs[i, j][:], op=MULT)
-            else:
-                ms = work.tile([P, 512], F32, name="ms", bufs=3)
-                nc.scalar.copy(out=ms[:], in_=banks["q", i, j][:])
-                nc.gpsimd.tensor_tensor(out=ot[:], in0=ms[:], in1=cs[i, j][:], op=MULT)
-            nc.sync.dma_start(out=out[P * i : P * i + P, 512 * j : 512 * j + 512], in_=ot[:])
-
-        def name_tile(s, a):
-            return ("k" if s < 4 else "q", 2 * (s % 4) + a)
-
-        def tile_of(n):
-            return ("k" if n < 8 else "q", n % 8)
-
-        run = {
-            "T": lambda n: transposes(*tile_of(n)),
-            "E": lambda n: evac(*tile_of(n)),
-            "Q": lambda n: quant1(*tile_of(n)),
-            "M": lambda n: project(*tile_of(n)),
-            "P": lambda n: empty(*tile_of(n)),
-            "D": lambda i: load_one(i),
-            "d": lambda s: load_pair(dq_sb, dq_bytes, s),
-            "a": lambda s: load_half(aq_sb, aq, s),
-            "b": lambda s: load_half(ak_sb, ak, s),
-            "w": lambda s: load_words("kq"[s], (wk_words, wq_words)[s]),
-            "R": lambda s: quant2("k" if s < 4 else "q", s % 4),
-            "W": lambda i: widen(i),
-            "u": lambda s: load_dqs(),
-            "s": lambda s: load_scales((nc.scalar, nc.sync)[s], "kq"[s], (wk_scales, wq_scales)[s]),
-            "v": lambda s: load_small(),
-            "h": lambda s: head_columns(),
-            "k": lambda s: permute("k"),
-            "q": lambda s: permute("q"),
-            "i": lambda s: inter("aq", s // 2, s % 2, aq_sb[s // 2]),
-            "I": lambda s: inter("aq", s // 2, s % 2, aq_sb[s // 2], "s"),
-            "j": lambda s: inter("ak", s // 2, s % 2, gk[s // 2]),
-            "J": lambda s: inter("ak", s // 2, s % 2, gk[s // 2], "s"),
-            "g": lambda s: gmul(s),
-            "x": lambda s: quant_a("aq", s),
-            "y": lambda s: quant_a("ak", s),
-            "C": lambda s: final_c(s // 2, s % 2),
-            "X": lambda s: final_x(s // 2, s % 2),
-            "Z": lambda s: final_x(s // 2, s % 2, "g"),
+        on_vector, on_scalar = nc.vector.tensor_copy, nc.scalar.copy
+        job_in_front = {
+            1: lambda: order_channels("k"),
+            2: lambda: order_channels("q"),
+            3: lambda: interleave("aq", 0, 1, on_vector),
+            4: lambda: multiply_g(0),
+            5: lambda: interleave("ak", 0, 1, on_vector),
+            7: lambda: interleave("aq", 1, 1, on_vector),
+            8: lambda: multiply_g(1),
+            9: lambda: interleave("ak", 1, 1, on_vector),
         }
-        order = """
-            D0 D1 u0 s0 d0 w0 D2 D3 d1 w1 a0 D4 s1 v0 D5 d2 b0 D6 D7 d3 a1 b1 T0 T1 E0 E1 W0 W1 T8 T9 E8 E9 k0 Q0 Q1 T2 T3 E2 E3 W2 W3 q0 Q8 Q9 M0 M1 P0 P1 I0 T10 T11 E10 E11 i1 Q2 Q3 h0 M8 M9 P8 P9 x0 R0 T4 T5 E4 E5 W4 W5 g0 Q10 Q11 M2 M3 P2 P3 j0 R4 T12 T13 E12 E13 j1 Q4 Q5 M10 M11 P10 P11 y0 R1 T6 T7 E6 E7 W6 W7 Q12 Q13 C0 M4 M5 P4 P5 I2 R5 T14 T15 E14 E15 i3 Q6 Q7 C2 X0 M12 M13 P12 P13 x1 R2 g1 Q14 Q15 C4 X2 M6 M7 P6 P7 j2 R6 j3 C6 X4 M14 M15 P14 P15 y1 R3 C8 X6 R7 C10 X8 C12 X10 C14 X12 C1 X14 C3 X1 C5 X3 C7 X5 C9 X7 C11 X9 C13 X11 C15 X13 X15
-        """
-        for token in order.split():
-            run[token[0]](int(token[1:]))
+        job_behind = {
+            2: lambda: interleave("aq", 0, 0, on_scalar),
+            3: lambda: quantize_tokens("aq", 0),
+            4: lambda: interleave("ak", 0, 0, on_vector),
+            5: lambda: quantize_tokens("ak", 0),
+            6: lambda: interleave("aq", 1, 0, on_scalar),
+            7: lambda: quantize_tokens("aq", 1),
+            8: lambda: interleave("ak", 1, 0, on_vector),
+            9: lambda: quantize_tokens("ak", 1),
+        }
+
+        for s in range(FIRST_PIECE_STEP + len(PIECES) + 1):
+            if s < len(CHAIN):
+                side, pair = CHAIN[s]
+                for i in (2 * pair, 2 * pair + 1):
+                    transpose(side, i)
+                for i in (2 * pair, 2 * pair + 1):
+                    collect(side, i)
+            if s + 1 < len(CHAIN) and CHAIN[s + 1][0] == "q":
+                pair = CHAIN[s + 1][1]
+                for i in (2 * pair, 2 * pair + 1):
+                    widen(i)
+            if s in job_in_front:
+                job_in_front[s]()
+            if 0 <= s - 1 < len(CHAIN):
+                quantize_first(*CHAIN[s - 1])
+            if 0 <= s - FIRST_PIECE_STEP < len(PIECES):
+                begin_piece(*PIECES[s - FIRST_PIECE_STEP])
+            if 0 <= s - FIRST_PIECE_STEP - 1 < len(PIECES):
+                finish_piece(*PIECES[s - FIRST_PIECE_STEP - 1])
+            if 0 <= s - 2 < len(CHAIN):
+                side, pair = CHAIN[s - 2]
+                if s - 2 == CHAIN.index(("q", 0)):
+                    spread_heads()
+                for i in (2 * pair, 2 * pair + 1):
+                    project(side, i)
+                for i in (2 * pair, 2 * pair + 1):
+                    round_projection(side, i)
+            if s in job_behind:
+                job_behind[s]()
+            if 0 <= s - 3 < len(CHAIN):
+                quantize_second(*CHAIN[s - 3])

import math
from contextlib import ExitStack

import concourse.mybir as mybir
from concourse.masks import make_identity

N_FEAT = 1024
WIDTH = 1024
CHANNELS = 512
HEADS = 4
TOKENS = 512
FLOPS = 2 * N_FEAT * (2 * WIDTH * CHANNELS + N_FEAT * CHANNELS + N_FEAT * TOKENS)

F32 = mybir.dt.float32
BF16 = mybir.dt.bfloat16
I32 = mybir.dt.int32
U32 = mybir.dt.uint32
U8 = mybir.dt.uint8
FP8 = mybir.dt.float8_e4m3fn
FP8X4 = mybir.dt.float8_e4m3fn_x4
FP4X4 = mybir.dt.float4_e2m1fn_x4
MULT = mybir.AluOpType.mult
COPY = mybir.ActivationFunctionType.Copy

P = 128
PACK = 4
HALF = 512
TILES = N_FEAT // P
CHAIN = [(side, pair) for pair in range(TILES // 2) for side in ("k", "q")]
PIECES = [(i, j) for j in range(2) for i in range(TILES)]
FIRST_PIECE_STEP = 6


def tile_featurepairqkscoreattribution_d2p_kernel(
    tc, dq_bytes, dq_scale, dk, wq_words, wq_scales, wk_words, wk_scales, head_w, aq, ak, g, out
):
    nc = tc.nc
    with ExitStack() as ctx:
        keep = ctx.enter_context(tc.tile_pool(name="keep", bufs=1))
        work = ctx.enter_context(tc.tile_pool(name="work", bufs=4))
        psum = ctx.enter_context(tc.psum_pool(name="psum", bufs=8))
        ctx.enter_context(tc.manual_schedule())

        ident = keep.tile([P, P], F32, name="ident")
        dk_in = [keep.tile([P, WIDTH], BF16, name="dk_in%d" % i) for i in range(TILES)]
        dq_in = [keep.tile([P, 2, WIDTH], U8, name="dq_in%d" % s) for s in range(TILES // 2)]
        dq_sc = keep.tile([P, 64], F32, name="dq_sc")
        aq_in = [keep.tile([P, PACK, HALF], BF16, name="aq_in%d" % h) for h in range(2)]
        ak_in = [keep.tile([P, PACK, HALF], BF16, name="ak_in%d" % h) for h in range(2)]
        g_in = keep.tile([P, PACK], BF16, name="g_in")
        head_in = keep.tile([P, HEADS], BF16, name="head_in")
        head_col = keep.tile([P, 1], F32, name="head_col")
        words_in, words, scales_in, scales = {}, {}, {}, {}
        for side in ("k", "q"):
            words_in[side] = keep.tile([P, 512], I32, name="words_in_" + side, align_bytes=64)
            words[side] = keep.tile([P, 512], I32, name="words_" + side, align_bytes=64)
            scales_in[side] = keep.tile([P, 256], I32, name="scales_in_" + side, align_bytes=64)
            scales[side] = keep.tile([P, 256], I32, name="scales_" + side, align_bytes=64)
        codes2, scales2 = {}, {}
        for name in ("k", "q", "aq", "ak"):
            codes2[name] = keep.tile([P, N_FEAT], U32, name="codes2_" + name, align_bytes=64)
            scales2[name] = keep.tile([P, N_FEAT], U8, name="scales2_" + name, align_bytes=64)

        for side in ("k", "q"):
            nc.vector.memset(scales_in[side][:], 0)
        make_identity(nc, ident[:])

        def load_dk(i):
            nc.sync.dma_start(out=dk_in[i][:], in_=dk[P * i : P * i + P, :])

        def load_dq(s):
            rows = dq_bytes[2 * P * s : 2 * P * s + 2 * P, :]
            nc.sync.dma_start(out=dq_in[s][:], in_=rows.rearrange("(a p) k -> p a k", p=P))

        def load_tokens(dst, src, h):
            cols = src[:, HALF * h : HALF * h + HALF]
            nc.sync.dma_start(out=dst[h][:], in_=cols.rearrange("(p t) w -> p t w", t=PACK))

        def load_words(side, src):
            nc.sync.dma_start(
                out=words_in[side][:].rearrange("p (g n) -> p g n", g=2),
                in_=src.bitcast(I32).rearrange("g p n -> p g n"),
            )

        def load_scales(queue, side, src):
            rows = src.bitcast(I32)
            for quad in range(4):
                queue.dma_start(
                    out=scales_in[side][32 * quad : 32 * quad + 4, :].rearrange("r (g n) -> r g n", g=2),
                    in_=rows[:, 4 * quad : 4 * quad + 4, :].rearrange("g r n -> r g n"),
                )

        load_dk(0)
        load_dq(0)
        nc.scalar.dma_start(out=dq_sc[:], in_=dq_scale.rearrange("i j -> (i j)").partition_broadcast(P))
        load_dk(1)
        load_scales(nc.scalar, "k", wk_scales)
        load_words("k", wk_words)
        load_dk(2)
        load_dk(3)
        load_dq(1)
        load_words("q", wq_words)
        load_scales(nc.sync, "q", wq_scales)
        load_tokens(aq_in, aq, 0)
        load_dk(4)
        nc.sync.dma_start(out=g_in[:], in_=g.rearrange("(p t) -> p t", t=PACK))
        nc.sync.dma_start(out=head_in[:], in_=head_w.partition_broadcast(P))
        load_dk(5)
        load_dq(2)
        load_tokens(ak_in, ak, 0)
        load_dk(6)
        load_dk(7)
        load_dq(3)
        load_tokens(aq_in, aq, 1)
        load_tokens(ak_in, ak, 1)

        def order_channels(side):
            for dst, src, run in ((words, words_in, 4), (scales, scales_in, 2)):
                nc.vector.tensor_copy(
                    out=dst[side][:].rearrange("p (t x w) -> p t x w", t=4, w=run),
                    in_=src[side][:].rearrange("p (x t w) -> p t x w", t=4, w=run),
                )

        def spread_heads():
            for h in range(HEADS):
                rows = slice(32 * h, 32 * h + 32)
                nc.scalar.copy(out=head_col[rows, 0:1], in_=head_in[rows, h : h + 1])

        dq_wide, first_in, first_q, second_in, bank_of = {}, {}, {}, {}, {}

        def widen(i):
            dq_wide[i] = work.tile([P, WIDTH], BF16, name="wide", bufs=8)
            by_pass = dq_wide[i][:].rearrange("p (g u m e) -> p g m u e", g=2, u=2, e=2)
            for j in range(8):
                nc.vector.tensor_scalar(
                    out=by_pass[:, j // 4, 32 * (j % 4) : 32 * (j % 4) + 32, :, :],
                    in0=dq_in[i // 2][:, i % 2, P * j : P * j + P].bitcast(FP8),
                    scalar1=dq_sc[:, 8 * i + j : 8 * i + j + 1],
                    scalar2=None,
                    op0=MULT,
                )

        def transpose(side, i):
            pairs = (dk_in[i] if side == "k" else dq_wide[i])[:].bitcast(F32)
            bank = psum.tile([P, HALF], F32, name="bank")
            for gg in range(2):
                for u in range(2):
                    at = P * (2 * gg + u)
                    if side == "k":
                        src = pairs[:, 2 * P * gg + u : 2 * P * gg + 2 * P : 2]
                    else:
                        src = pairs[:, at : at + P]
                    nc.tensor.transpose(bank[:, at : at + P], src, ident[:])
            bank_of[side, i] = bank

        def collect(side, i):
            if (side, i // 2) not in first_in:
                first_in[side, i // 2] = work.tile([P, 2048], BF16, name="first_in", bufs=4, align_bytes=64)
            dst = first_in[side, i // 2][:, 1024 * (i % 2) : 1024 * (i % 2) + 1024]
            nc.scalar.copy(
                out=dst.bitcast(F32).rearrange("p (g f u) -> p g f u", g=2, u=2),
                in_=bank_of[side, i][:].rearrange("p (g u f) -> p g f u", g=2, u=2),
            )

        def quantize_first(side, s):
            codes = work.tile([P, 512], U32, name="codes1", bufs=6, align_bytes=64)
            sc = work.tile([P, 512], U8, name="scales1", bufs=6, align_bytes=64)
            nc.vector.quantize_mx(out=codes[:].bitcast(FP8X4), scales=sc[:], in_=first_in[side, s][:])
            first_q[side, s] = (codes, sc)

        def project(side, i):
            codes, sc = first_q[side, i // 2]
            bank = psum.tile([P, HALF], F32, name="bank")
            for t in range(PACK):
                for gg in range(2):
                    at = P * (2 * (i % 2) + gg)
                    nc.tensor.matmul_mx(
                        out=bank[:, P * t : P * t + P],
                        lhsT=words[side][:, 128 * t + 64 * gg : 128 * t + 64 * gg + 64].bitcast(FP4X4),
                        lhsT_scale=scales[side][:, 64 * t + 32 * gg : 64 * t + 32 * gg + 32].bitcast(U8),
                        rhs=codes[:, at : at + P].bitcast(FP8X4),
                        rhs_scale=sc[:, at : at + P],
                        start=(gg == 0),
                        stop=(gg == 1),
                    )
            bank_of[side, i] = bank

        def round_projection(side, i):
            if (side, i // 2) not in second_in:
                second_in[side, i // 2] = work.tile([P, 2, HALF], BF16, name="second_in", bufs=4, align_bytes=64)
            dst = second_in[side, i // 2][:, i % 2, :].rearrange("p (f t) -> p f t", t=PACK)
            src = bank_of[side, i][:].rearrange("p (t f) -> p f t", t=PACK)
            if side == "k":
                nc.scalar.copy(out=dst, in_=src)
            else:
                nc.scalar.activation(out=dst, in_=src, func=COPY, scale=head_col[:, 0:1])

        def quantize_second(side, s):
            cols = slice(2 * P * s, 2 * P * s + 2 * P)
            nc.vector.quantize_mx(
                out=codes2[side][:, cols].bitcast(FP8X4),
                scales=scales2[side][:, cols],
                in_=second_in[side, s][:].rearrange("p a c -> p (a c)"),
            )

        ak_g, side_by_side = {}, {}

        def multiply_g(h):
            ak_g[h] = work.tile([P, PACK, HALF], BF16, name="ak_g", bufs=2)
            for t in range(PACK):
                nc.vector.tensor_scalar(
                    out=ak_g[h][:, t, :], in0=ak_in[h][:, t, :], scalar1=g_in[:, t : t + 1], scalar2=None, op0=MULT
                )

        def interleave(name, h, part, copy):
            if (name, h) not in side_by_side:
                side_by_side[name, h] = work.tile([P, 2048], BF16, name="side_by_side", bufs=4, align_bytes=64)
            src = aq_in[h] if name == "aq" else ak_g[h]
            copy(
                out=side_by_side[name, h][:, 1024 * part : 1024 * part + 1024].rearrange(
                    "p (c i t) -> p c t i", i=4, t=PACK
                ),
                in_=src[:, :, 256 * part : 256 * part + 256].rearrange("p t (c i) -> p c t i", i=4),
            )

        def quantize_tokens(name, h):
            cols = slice(HALF * h, HALF * h + HALF)
            nc.vector.quantize_mx(
                out=codes2[name][:, cols].bitcast(FP8X4), scales=scales2[name][:, cols], in_=side_by_side[name, h][:]
            )

        divisor = 1.0 / (TOKENS * math.sqrt(CHANNELS // HEADS))
        c_part = {}

        def product(rows, cols, i, j):
            bank = psum.tile([P, HALF], F32, name="bank")
            nc.tensor.matmul_mx(
                out=bank[:],
                lhsT=codes2[rows][:, P * i : P * i + P].bitcast(FP8X4),
                lhsT_scale=scales2[rows][:, P * i : P * i + P],
                rhs=codes2[cols][:, HALF * j : HALF * j + HALF].bitcast(FP8X4),
                rhs_scale=scales2[cols][:, HALF * j : HALF * j + HALF],
                start=True,
                stop=True,
            )
            return bank

        def begin_piece(i, j):
            bank = product("aq", "ak", i, j)
            c_part[i, j] = work.tile([P, HALF], F32, name="c_part", bufs=8)
            nc.scalar.activation(out=c_part[i, j][:], in_=bank[:], func=COPY, scale=divisor)

        def finish_piece(i, j):
            bank = product("q", "k", i, j)
            piece = work.tile([P, HALF], F32, name="piece", bufs=8)
            nc.vector.tensor_tensor(out=piece[:], in0=bank[:], in1=c_part[i, j][:], op=MULT)
            nc.sync.dma_start(out=out[P * i : P * i + P, HALF * j : HALF * j + HALF], in_=piece[:])

        on_vector, on_scalar = nc.vector.tensor_copy, nc.scalar.copy
        job_in_front = {
            1: lambda: order_channels("k"),
            2: lambda: order_channels("q"),
            3: lambda: interleave("aq", 0, 1, on_vector),
            4: lambda: multiply_g(0),
            5: lambda: interleave("ak", 0, 1, on_vector),
            7: lambda: interleave("aq", 1, 1, on_vector),
            8: lambda: multiply_g(1),
            9: lambda: interleave("ak", 1, 1, on_vector),
        }
        job_behind = {
            2: lambda: interleave("aq", 0, 0, on_scalar),
            3: lambda: quantize_tokens("aq", 0),
            4: lambda: interleave("ak", 0, 0, on_vector),
            5: lambda: quantize_tokens("ak", 0),
            6: lambda: interleave("aq", 1, 0, on_scalar),
            7: lambda: quantize_tokens("aq", 1),
            8: lambda: interleave("ak", 1, 0, on_vector),
            9: lambda: quantize_tokens("ak", 1),
        }

        for s in range(FIRST_PIECE_STEP + len(PIECES) + 1):
            if s < len(CHAIN):
                side, pair = CHAIN[s]
                for i in (2 * pair, 2 * pair + 1):
                    transpose(side, i)
                for i in (2 * pair, 2 * pair + 1):
                    collect(side, i)
            if s + 1 < len(CHAIN) and CHAIN[s + 1][0] == "q":
                pair = CHAIN[s + 1][1]
                for i in (2 * pair, 2 * pair + 1):
                    widen(i)
            if s in job_in_front:
                job_in_front[s]()
            if 0 <= s - 1 < len(CHAIN):
                quantize_first(*CHAIN[s - 1])
            if 0 <= s - FIRST_PIECE_STEP < len(PIECES):
                begin_piece(*PIECES[s - FIRST_PIECE_STEP])
            if 0 <= s - FIRST_PIECE_STEP - 1 < len(PIECES):
                finish_piece(*PIECES[s - FIRST_PIECE_STEP - 1])
            if 0 <= s - 2 < len(CHAIN):
                side, pair = CHAIN[s - 2]
                if s - 2 == CHAIN.index(("q", 0)):
                    spread_heads()
                for i in (2 * pair, 2 * pair + 1):
                    project(side, i)
                for i in (2 * pair, 2 * pair + 1):
                    round_projection(side, i)
            if s in job_behind:
                job_behind[s]()
            if 0 <= s - 3 < len(CHAIN):
                quantize_second(*CHAIN[s - 3])
